import numpy as np, ml_dtypes
CORES = [4,20,36,44,92,100,108,116,3,19,35,43,91,99,107,115]
N = 16
C = 128
SIGN = [[1,1,1,1,1,1,1,1,1,1,1,1,1,1,1,1],[1,-1,1,-1,1,-1,1,-1,1,-1,1,-1,1,-1,1,-1],[1,1,-1,-1,1,1,-1,-1,1,1,-1,-1,1,1,-1,-1],[1,-1,-1,1,1,-1,-1,1,1,-1,-1,1,1,-1,-1,1],[1,1,1,1,-1,-1,-1,-1,1,1,1,1,-1,-1,-1,-1],[1,-1,1,-1,-1,1,-1,1,1,-1,1,-1,-1,1,-1,1],[1,1,-1,-1,-1,-1,1,1,1,1,-1,-1,-1,-1,1,1],[1,-1,-1,1,-1,1,1,-1,1,-1,-1,1,-1,1,1,-1],[1,1,1,1,1,1,1,1,-1,-1,-1,-1,-1,-1,-1,-1],[1,-1,1,-1,1,-1,1,-1,-1,1,-1,1,-1,1,-1,1],[1,1,-1,-1,1,1,-1,-1,-1,-1,1,1,-1,-1,1,1],[1,-1,-1,1,1,-1,-1,1,-1,1,1,-1,-1,1,1,-1],[1,1,1,1,-1,-1,-1,-1,-1,-1,-1,-1,1,1,1,1],[1,-1,1,-1,-1,1,-1,1,-1,1,-1,1,1,-1,1,-1],[1,1,-1,-1,-1,-1,1,1,-1,-1,1,1,1,1,-1,-1],[1,-1,-1,1,-1,1,1,-1,-1,1,1,-1,1,-1,-1,1]]
def setup_inputs(rng):
    return {"x": rng.standard_normal((N, 128, C), dtype=np.float32).astype(ml_dtypes.bfloat16), "w": (rng.standard_normal((N, 128, 128), dtype=np.float32) / 11).astype(ml_dtypes.bfloat16)}
def setup_inputs_big(rng):
    d = setup_inputs(rng)
    for k in ("x", "w"): d[k] = (d[k].astype(np.float32) * 1024.0).astype(d[k].dtype)
    return d
def setup_inputs_small(rng):
    d = setup_inputs(rng)
    for k in ("x", "w"): d[k] = (d[k].astype(np.float32) * (1 / 1024.0)).astype(d[k].dtype)
    return d
def setup_inputs_apart(rng):
    d = setup_inputs(rng)
    f = (10.0 ** rng.permutation(np.linspace(-1.5, 1.5, N))).astype(np.float32).reshape(N, 1, 1)
    for k in ("x", "w"): d[k] = (d[k].astype(np.float32) * f).astype(d[k].dtype)
    return d
def reference(x, w):
    X = x.astype(np.float64)
    y = np.stack([w[r].astype(np.float64).T @ sum(SIGN[r][j] * X[j] for j in range(N)) for r in range(N)])
    return {"y": y.astype(ml_dtypes.bfloat16)}

from concourse.bass import DstId, RemoteDMATransfer
from concourse.mybir import AluOpType

N = 16
C = 128
NSETS = 3
MAXC = 6

SCRATCH = {
    "xin": ("sbuf", [128, N * C], "bfloat16"),
    "pin": ("sbuf", [128, NSETS * C], "bfloat16"),
    "pout": ("sbuf", [128, MAXC * C], "bfloat16"),
    "wp": ("sbuf", [128, C], "bfloat16"),
    "wn": ("sbuf", [128, C], "bfloat16"),
    "zero": ("sbuf", [128, C], "bfloat16"),
    "zp": ("sbuf", [128, C + 1], "bfloat16"),
    "idp": ("sbuf", [128, C], "bfloat16"),
    "idn": ("sbuf", [128, C], "bfloat16"),
    "ybf": ("sbuf", [128, C], "bfloat16"),
    "idd": ("dram", [C + 1, 128], "bfloat16"),
    "psy": ("psum", [128, 512], "float32"),
}
for _c in range(MAXC):
    SCRATCH["ps%d" % _c] = ("psum", [128, 512], "float32")

SEMAPHORES = (["ld", "lw", "zs", "zz", "wr", "i1", "i2", "ir", "yd", "yc", "st", "sent"]
              + ["a%d" % j for j in range(N)] + ["p%d" % s for s in range(NSETS)]
              + ["cm%d" % c for c in range(MAXC)] + ["pc%d" % c for c in range(MAXC)])


def popcount(m):
    return bin(m).count("1")


def make_plan(cores, sign, topo):
    n = len(cores)
    chips = []
    for c in cores:
        if topo.chip(c) not in chips:
            chips.append(topo.chip(c))
    planes = []
    for ch in chips:
        for p in planes:
            if topo.same_plane(p[0], ch):
                p.append(ch)
                break
        else:
            planes.append([ch])
    on_chip = {ch: [r for r in range(n) if topo.chip(cores[r]) == ch] for ch in chips}

    def gate(r):
        return all(topo.may_write(cores[r], cores[q]) for q in range(n) if q != r)

    sets = []
    for p in planes:
        rest = list(p)
        while rest:
            k = len(rest) if len(rest) <= 3 else 2
            part, rest = rest[:k], rest[k:]
            members = [r for ch in part for r in on_chip[ch]]
            agents = [r for r in members if gate(r)] if k == 3 else list(members)
            sets.append({"members": members, "agents": agents})

    hop1 = {r: [] for r in range(n)}
    for s in sets:
        for r in s["members"]:
            hop1[r] = [a for a in s["agents"] if a != r]

    combos = {r: [] for r in range(n)}
    terms = {r: [] for r in range(n)}
    for si, s in enumerate(sets):
        mem = s["members"]
        load = {a: 0 for a in s["agents"]}
        need = [r for r in range(n) if r not in s["agents"]]
        need.sort(key=lambda r: (sum(topo.may_write(cores[a], cores[r]) for a in s["agents"]),
                                 not any(topo.mates(topo.chip(cores[a]), topo.chip(cores[r])) for a in s["agents"])))
        for a in s["agents"]:
            for j in mem:
                terms[a].append(("x", j, sign[a][j]))
        for r in need:
            sg = sign[r][mem[0]]
            co = tuple(sg * sign[r][j] for j in mem)
            ok = [a for a in s["agents"] if topo.may_write(cores[a], cores[r])]
            home = [a for a in ok if topo.chip(cores[a]) == topo.chip(cores[r])]
            if home:
                a = home[0]
            else:
                def key(a):
                    has = any(c[0] == si and c[1] == co for c in combos[a])
                    mate = topo.mates(topo.chip(cores[a]), topo.chip(cores[r]))
                    return (load[a] - (2 if mate else 0), not has)
                a = min(ok, key=key)
                load[a] += 1
            for c in combos[a]:
                if c[0] == si and c[1] == co:
                    c[2].append(r)
                    break
            else:
                combos[a].append([si, co, [r]])
            terms[r].append(("p", si, sg, a))
    for a in range(n):
        combos[a].sort(key=lambda c: -sum(topo.chip(cores[r]) != topo.chip(cores[a]) for r in c[2]))
    place = {}
    for a in range(n):
        k = 0
        for c in combos[a]:
            k += sum(topo.chip(cores[r]) != topo.chip(cores[a]) for r in c[2])
            for r in c[2]:
                place[(c[0], r)] = k
    for r in range(n):
        terms[r].sort(key=lambda t: place[(t[1], r)] if t[0] == "p" else -1)
    return sets, hop1, combos, terms


def rank_program(g, core, T, topo):
    rank = T.rank_of(core)
    if rank is None:
        return
    cores = T.cores
    sign = T.tables["SIGN"]
    sets, hop1, combos, terms = make_plan(cores, sign, topo)
    sem = T.sem

    def mask_for(src, dst):
        if topo.chip(src) != topo.chip(dst):
            return topo.mask(src, dst)
        other = [c for c in cores if topo.chip(c) != topo.chip(src)][0]
        return topo.mask(src, dst) & ~topo.mask(src, other)

    def xs(j):
        return T.xin[:, j * C:(j + 1) * C]

    sent = [0]

    def send(src_ap, dst_ap, dests, rsem):
        off = [d for d in dests if topo.chip(cores[d]) != topo.chip(core)]
        on = [d for d in dests if topo.chip(cores[d]) == topo.chip(core)]
        for grp in (off, on):
            if not grp:
                continue
            m = mask_for(core, cores[grp[0]])
            ids = [DstId(rid=topo.addr(cores[d])[0], pnc=topo.addr(cores[d])[1]) for d in grp]
            g.remote_dma_fused([RemoteDMATransfer(dst_ids=ids, dma_engine_mask=m, remote_sem=rsem,
                                                  srcs=[src_ap], dsts=[dst_ap for _ in grp], alu_op=0)],
                               local_sem=sem.sent)
            sent[0] += popcount(m)

    mine = combos[rank]
    agent = len(mine) > 0
    myset = [s for s in sets if rank in s["members"]][0]

    g.sync.dma_start(xs(rank), T.x[:, :]).then_inc(sem.ld, 16)
    g.sync.dma_start(T.wp[:, :], T.w[:, :]).then_inc(sem.lw, 16)
    if agent:
        g.vector.memset(T.zp[:, 1:C + 1], 0.0).then_inc(sem.zs, 1)
        g.vector.memset(T.zp[:, 0:1], 1.0).then_inc(sem.zs, 1)
        g.scalar.wait_ge(sem.zs, 2)
        g.scalar.dma_start(T.idd[:, :], T.zp[:, :]).then_inc(sem.i1, 16)
        g.scalar.wait_ge(sem.i1, 16)
        g.scalar.dma_start(T.idp[:, :], T.idd[0:128, :]).then_inc(sem.i2, 16)
    g.vector.memset(T.zero[:, :], 0.0).then_inc(sem.zz, 1)
    g.vector.wait_ge(sem.zz, 1)
    g.vector.wait_ge(sem.lw, 16)
    g.vector.tensor_tensor(T.wn[:, :], T.zero[:, :], T.wp[:, :], AluOpType.subtract).then_inc(sem.wr, 1)
    if agent:
        g.vector.wait_ge(sem.i2, 16)
        g.vector.tensor_tensor(T.idn[:, :], T.zero[:, :], T.idp[:, :], AluOpType.subtract).then_inc(sem.ir, 1)

    g.wait_ge(sem.ld, 16)
    send(xs(rank), xs(rank), hop1[rank], sem["a%d" % rank])

    def wait_x(j):
        if j == rank:
            g.tensor.wait_ge(sem.ld, 16)
        else:
            g.tensor.wait_ge(sem["a%d" % j], popcount(mask_for(cores[j], core)))

    holds = [t[1] for t in terms[rank] if t[0] == "x"]
    holds.sort(key=lambda j: (j != rank, topo.chip(cores[j]) != topo.chip(core)))
    if agent:
        g.tensor.wait_ge(sem.i2, 16)
        g.tensor.wait_ge(sem.ir, 1)
        mem = myset["members"]
        for k, j in enumerate(holds):
            wait_x(j)
            for c, (si, co, dests) in enumerate(mine):
                lhs = T.idp if co[mem.index(j)] > 0 else T.idn
                mm = g.tensor.matmul(T["ps%d" % c][:, 0:C], lhs[:, :], xs(j), k == 0, k == len(holds) - 1)
                if k == len(holds) - 1:
                    mm.then_inc(sem["cm%d" % c], 1)
        for c, (si, co, dests) in enumerate(mine):
            po = T.pout[:, c * C:(c + 1) * C]
            g.vector.wait_ge(sem["cm%d" % c], 1)
            g.vector.tensor_copy(po, T["ps%d" % c][:, 0:C]).then_inc(sem["pc%d" % c], 1)
            g.wait_ge(sem["pc%d" % c], 1)
            send(po, T.pin[:, si * C:(si + 1) * C], dests, sem["p%d" % si])

    g.tensor.wait_ge(sem.lw, 16)
    g.tensor.wait_ge(sem.wr, 1)
    sgn = {t[1]: t[2] for t in terms[rank] if t[0] == "x"}
    todo = [("x", j, sgn[j], None) for j in holds] + [t for t in terms[rank] if t[0] == "p"]
    for k, t in enumerate(todo):
        if t[0] == "x":
            rhs = xs(t[1])
        else:
            g.tensor.wait_ge(sem["p%d" % t[1]], popcount(mask_for(cores[t[3]], core)))
            rhs = T.pin[:, t[1] * C:(t[1] + 1) * C]
        lhs = T.wp if t[2] > 0 else T.wn
        mm = g.tensor.matmul(T.psy[:, 0:C], lhs[:, :], rhs, k == 0, k == len(todo) - 1)
        if k == len(todo) - 1:
            mm.then_inc(sem.yd, 1)

    g.vector.wait_ge(sem.yd, 1)
    g.vector.tensor_copy(T.ybf[:, :], T.psy[:, 0:C]).then_inc(sem.yc, 1)
    g.sync.wait_ge(sem.yc, 1)
    g.sync.dma_start(T.y[:, :], T.ybf[:, :]).then_inc(sem.st, 16)
    g.sync.wait_ge(sem.st, 16)
    g.wait_ge(sem.sent, sent[0])
